import numpy as np
import ml_dtypes


def mxq(x, axis, fmt="e4m3"):
    dtype, down = {"e4m3": (ml_dtypes.float8_e4m3fn, 7), "e5m2": (ml_dtypes.float8_e5m2, 14)}[fmt]
    v = np.moveaxis(np.asarray(x, np.float32).astype(ml_dtypes.bfloat16).astype(np.float64), axis, -1)
    blocks = v.reshape(v.shape[:-1] + (-1, 32))
    amax = np.abs(blocks).max(-1, keepdims=True)
    byte = np.maximum(np.where(amax > 0, np.frexp(amax)[1] - 1 + 127, 0) - down, 1)
    scale = np.exp2(byte - 127.0)
    codes = (blocks / scale).astype(np.float32).astype(dtype).astype(np.float64)
    return np.moveaxis((codes * scale).reshape(v.shape), -1, axis)


WIDE = False


def mx_kscale(k):
    if not WIDE:
        return np.ones(k)
    levels = np.array([10, -10, 5, -5, 0])
    if k % 512:
        return np.exp2(np.random.permutation(np.resize(levels, k // 32))).repeat(32)
    a = np.empty((k // 512, 16))
    for p in range(k // 512):
        a[p, :8] = np.random.permutation(np.resize(levels, 8))
        for g in range(8):
            far = levels[np.abs(levels - a[p, g]) >= 10]
            a[p, g + 8] = far[np.random.randint(len(far))]
    return np.exp2(a.ravel()).repeat(32)


def f64(x):
    return np.asarray(x).astype(np.float64)


E2M1 = np.array([0.0, 0.5, 1.0, 1.5, 2.0, 3.0, 4.0, 6.0, -0.0, -0.5, -1.0, -1.5, -2.0, -3.0, -4.0, -6.0])


def pack_weight(w, fmt):
    k, n = w.shape
    w = f64(np.asarray(w, np.float32).astype(ml_dtypes.bfloat16)).reshape(k // 32, 32, n)
    amax = np.abs(w).max(1)
    if fmt == "e4m3":
        byte = np.frexp(amax)[1] - 1 + 127 - 7
    else:
        mant, ex = np.frexp(amax / 6.0)
        byte = np.where(mant > 0.5, ex, ex - 1) + 127
    byte = np.clip(np.where(amax > 0, byte, 1), 1, 254)
    scaled = (w * np.exp2(127.0 - byte)[:, None, :]).reshape(k, n).astype(np.float32)
    by_word = np.ascontiguousarray(scaled.reshape(k // 512, 128, 4, n).transpose(0, 1, 3, 2))
    if fmt == "e4m3":
        words = by_word.astype(ml_dtypes.float8_e4m3fn).view(np.uint8)
    else:
        c = by_word.astype(ml_dtypes.float4_e2m1fn).view(np.uint8) & 0xF
        words = (c[..., 0::2] | (c[..., 1::2] << 4)).reshape(k // 512, 128, 2 * n)
    return np.ascontiguousarray(words), np.ascontiguousarray(byte.astype(np.uint8).reshape(k // 512, 16, n))


def unpack_weight(words, scales, fmt):
    g, _, n = scales.shape
    words = np.ascontiguousarray(words).reshape(g, 128, n, -1)
    if fmt == "e4m3":
        vals = words.view(ml_dtypes.float8_e4m3fn).astype(np.float64)
    else:
        nib = np.empty((g, 128, n, 4), np.uint8)
        nib[..., 0::2] = words & 0xF
        nib[..., 1::2] = words >> 4
        vals = E2M1[nib]
    vals = vals * np.repeat(np.exp2(scales.astype(np.float64) - 127.0), 8, axis=1)[..., None]
    return vals.transpose(0, 1, 3, 2).reshape(g * 512, n)


def bf(x):
    return np.asarray(x, np.float32).astype(ml_dtypes.bfloat16)


def planes(Y):
    r, m = Y.shape
    b = f64(bf(Y)).reshape(r // 32, 32, m)
    amax = np.abs(b).max(1)
    byte = np.clip(np.where(amax > 0, np.frexp(amax)[1] - 1 + 127 - 7, 1), 1, 254)
    codes = (b * np.exp2(127.0 - byte)[:, None, :]).reshape(r, m).astype(np.float32).astype(ml_dtypes.float8_e4m3fn).view(np.uint8)
    words = codes.reshape(r // 512, 128, 4, m).transpose(0, 1, 3, 2)
    return np.ascontiguousarray(words), np.ascontiguousarray(byte.astype(np.uint8).reshape(r // 512, 16, m))


K, L, T, N = 1024, 1024, 512, 512


def setup_inputs():
    n = np.random.standard_normal
    fk = mx_kscale(K)
    fl = mx_kscale(L)
    xtp = pack_weight(n((K, T)) / fk[:, None], "e2m1")
    wap = pack_weight(n((K, N)) * 1 / np.sqrt(K) * fk[:, None], "e4m3")
    wqp = pack_weight(n((L, N)) * 1 / np.sqrt(L) * fl[:, None], "e2m1")
    return {
        "xt_words": xtp[0],
        "xt_scales": xtp[1],
        "wa_words": wap[0],
        "wa_scales": wap[1],
        "xq": (n((L, T)) / fl[:, None]).astype(np.float32),
        "wq_words": wqp[0],
        "wq_scales": wqp[1],
        "wd": (n((K, N)) * 1 / np.sqrt(K) * fk[:, None]).astype(np.float32),
        "sh": (np.random.uniform(0.1, 0.4, (N, 1))).astype(np.float32),
    }


def reference(xt_words, xt_scales, wa_words, wa_scales, xq, wq_words, wq_scales, wd, sh):
    xtu = unpack_weight(xt_words, xt_scales, "e2m1")
    wau = unpack_weight(wa_words, wa_scales, "e4m3")
    wqu = unpack_weight(wq_words, wq_scales, "e2m1")
    xqq = mxq(f64(xq), 0, "e4m3")
    p = wau.T @ xtu + wqu.T @ xqq
    wdq = mxq(f64(wd), 0, "e4m3")
    d = wdq.T @ xtu
    y = p / (1.0 + np.maximum(d, 0.0)) + f64(sh) * d
    words, scales = planes(y)
    return y, words, scales

@@ -1,0 +1,281 @@
+from contextlib import ExitStack
+
+import concourse.mybir as mybir
+
+K, L, T, N = 1024, 1024, 512, 512
+FLOPS = 3 * 2 * K * N * T
+
+F32 = mybir.dt.float32
+BF16 = mybir.dt.bfloat16
+I32 = mybir.dt.int32
+U32 = mybir.dt.uint32
+U8 = mybir.dt.uint8
+FP8X4 = mybir.dt.float8_e4m3fn_x4
+FP4X4 = mybir.dt.float4_e2m1fn_x4
+ALU = mybir.AluOpType
+ACT = mybir.ActivationFunctionType
+
+P = 128
+PACK = 4
+PASSES = 2
+CH = 128
+CHUNKS = T // CH
+
+
+def tile_mix_sum_divided_by_drive_pl_kernel(
+    tc, xt_words, xt_scales, wa_words, wa_scales, xq, wq_words, wq_scales, wd, sh, out_0, out_1, out_2
+):
+    nc = tc.nc
+    with ExitStack() as ctx:
+        sb = ctx.enter_context(tc.tile_pool(name="sb", bufs=1))
+        ps = ctx.enter_context(tc.psum_pool(name="ps", bufs=1))
+
+        def tile(name, shape, dtype):
+            return sb.tile(shape, dtype, name=name, align_bytes=64)
+
+        xt = tile("xt", [P, PASSES, 2 * T], U8)
+        xt_sc = tile("xt_sc", [P, PASSES, T], U8)
+        wq_raw = tile("wq_raw", [P, PASSES, 2 * N], U8)
+        wq_sc_raw = tile("wq_sc_raw", [P, PASSES, N], U8)
+        wa_raw = tile("wa_raw", [P, PASSES, N], I32)
+        wa_sc_raw = tile("wa_sc_raw", [P, PASSES, N], U8)
+        wq = [tile("wq%d" % z, [P, 2 * N], U8) for z in range(PASSES)]
+        wa = [tile("wa%d" % z, [P, N], U32) for z in range(PASSES)]
+        wq_sc = tile("wq_sc", [P, PASSES, N], U8)
+        wa_sc = tile("wa_sc", [P, PASSES, N], U8)
+        share = tile("share", [P, PACK], F32)
+        warm_in = tile("warm_in", [P, 1], F32)
+        warm_out = tile("warm_out", [P, 1], F32)
+
+        wd_pieces = [(0, 0, N), (1, 0, N // 2), (1, N // 2, N // 2)]
+        wd_raw = [tile("wd_raw%d" % i, [P, PACK, w], F32) for i, (z, n0, w) in enumerate(wd_pieces)]
+        wd_bf = [tile("wd_bf%d" % z, [P, PACK * N], BF16) for z in range(PASSES)]
+        wd_c = [tile("wd_c%d" % z, [P, N], U32) for z in range(PASSES)]
+        wd_sc = [tile("wd_sc%d" % z, [P, N], U8) for z in range(PASSES)]
+
+        xq_pieces = [(0, 0, 256), (1, 0, 256), (0, 256, 256), (1, 256, 128), (1, 384, 128)]
+        xq_raw = [tile("xq_raw%d" % i, [P, PACK, w], F32) for i, (z, t0, w) in enumerate(xq_pieces)]
+        xq_bf = [tile("xq_bf%d" % i, [P, PACK * w], BF16) for i, (z, t0, w) in enumerate(xq_pieces)]
+        xq_c = [tile("xq_c%d" % i, [P, w], U32) for i, (z, t0, w) in enumerate(xq_pieces)]
+        xq_sc = [tile("xq_sc%d" % i, [P, w], U8) for i, (z, t0, w) in enumerate(xq_pieces)]
+
+        pos = [tile("pos%d" % c, [P, PACK * CH], F32) for c in range(CHUNKS)]
+        root = [tile("root%d" % c, [P, PACK * CH], F32) for c in range(CHUNKS)]
+        gain = [tile("gain%d" % c, [P, PACK * CH], F32) for c in range(CHUNKS)]
+        quot = [tile("quot%d" % c, [P, PACK * CH], F32) for c in range(CHUNKS)]
+        y = [tile("y%d" % c, [P, PACK, CH], F32) for c in range(CHUNKS)]
+        y_bf = [tile("y_bf%d" % c, [P, PACK * CH], BF16) for c in range(CHUNKS)]
+        y_c = tile("y_c", [P, T], U32)
+        y_sc = tile("y_sc", [P, T], U8)
+
+        d_ps = [ps.tile([P, PACK * CH], F32, name="d_ps%d" % c) for c in range(CHUNKS)]
+        p_ps = [ps.tile([P, PACK * CH], F32, name="p_ps%d" % c) for c in range(CHUNKS)]
+
+        def load_scales(queue, plane, scales):
+            for q in range(4):
+                queue.dma_start(
+                    out=plane[32 * q : 32 * q + 4, :, :].bitcast(I32),
+                    in_=scales[:, 4 * q : 4 * q + 4, :].rearrange("z r c -> r z c").bitcast(I32),
+                )
+
+        def load_wd(i):
+            z, n0, w = wd_pieces[i]
+            rows = wd[512 * z : 512 * (z + 1), :].rearrange("(p j) n -> p j n", j=PACK)
+            nc.sync.dma_start(out=wd_raw[i][:], in_=rows[:, :, n0 : n0 + w])
+
+        def load_xq(i):
+            z, t0, w = xq_pieces[i]
+            rows = xq[512 * z : 512 * (z + 1), :].rearrange("(p j) t -> p j t", j=PACK)
+            nc.sync.dma_start(out=xq_raw[i][:], in_=rows[:, :, t0 : t0 + w])
+
+        def copy_on(engine, out, in_):
+            if engine == "vector":
+                nc.vector.tensor_copy(out=out, in_=in_)
+            else:
+                nc.scalar.copy(out=out, in_=in_)
+
+        def round_wd(engine, i, m0, m1):
+            z, n0, w = wd_pieces[i]
+            src = wd_raw[i][:].rearrange("p j (m r) -> p m j r", r=PACK)[:, m0:m1, :, :]
+            dst = wd_bf[z][:].rearrange("p (r m j) -> p m j r", r=PACK, j=PACK)
+            copy_on(engine, dst[:, n0 // PACK + m0 : n0 // PACK + m1, :, :], src)
+
+        def interleave(engine, dst, src):
+            copy_on(
+                engine,
+                dst.rearrange("p (c i j) -> p c j i", i=4, j=PACK),
+                src.rearrange("p j (c i) -> p c j i", i=4),
+            )
+
+        def quantize(codes, scales, values):
+            nc.vector.quantize_mx(out=codes.bitcast(FP8X4), scales=scales, in_=values)
+
+        def deal_scales(dst, src):
+            nc.vector.tensor_copy(
+                out=dst[:].rearrange("p z (r a b) -> p z a r b", r=PACK, b=16),
+                in_=src[:].rearrange("p z (a b r) -> p z a r b", r=PACK, b=16),
+            )
+
+        def deal_wq(z):
+            nc.vector.tensor_copy(
+                out=wq[z][:].rearrange("p (r a b e) -> p a r b e", r=PACK, b=8, e=2),
+                in_=wq_raw[:, z, :].rearrange("p (a b r e) -> p a r b e", r=PACK, b=8, e=2),
+            )
+
+        def deal_wa(z):
+            nc.vector.tensor_copy(
+                out=wa[z][:].bitcast(I32).rearrange("p (r a b) -> p a r b", r=PACK, b=4),
+                in_=wa_raw[:, z, :].rearrange("p (a b r) -> p a r b", r=PACK, b=4),
+            )
+
+        def by_tokens(bank, c, z, codes, scales, start, stop):
+            for r in range(PACK):
+                nc.tensor.matmul_mx(
+                    out=bank[:, CH * r : CH * (r + 1)],
+                    lhsT=codes[:, P * r : P * (r + 1)].bitcast(FP8X4),
+                    lhsT_scale=scales[:, P * r : P * (r + 1)],
+                    rhs=xt[:, z, 2 * CH * c : 2 * CH * (c + 1)].bitcast(FP4X4),
+                    rhs_scale=xt_sc[:, z, CH * c : CH * (c + 1)],
+                    start=(start and r == 0),
+                    stop=(stop and r == PACK - 1),
+                )
+
+        def by_second_input(c, z, stop):
+            i = [k for k, (zz, t0, w) in enumerate(xq_pieces) if zz == z and t0 <= CH * c < t0 + w][0]
+            t = CH * c - xq_pieces[i][1]
+            for r in range(PACK):
+                nc.tensor.matmul_mx(
+                    out=p_ps[c][:, CH * r : CH * (r + 1)],
+                    lhsT=wq[z][:, 2 * P * r : 2 * P * (r + 1)].bitcast(FP4X4),
+                    lhsT_scale=wq_sc[:, z, P * r : P * (r + 1)],
+                    rhs=xq_c[i][:, t : t + CH].bitcast(FP8X4),
+                    rhs_scale=xq_sc[i][:, t : t + CH],
+                    start=False,
+                    stop=(stop and r == PACK - 1),
+                )
+
+        def sum_products(c):
+            by_tokens(p_ps[c], c, 0, wa[0], wa_sc[:, 0, :], True, False)
+            by_tokens(p_ps[c], c, 1, wa[1], wa_sc[:, 1, :], False, False)
+            by_second_input(c, 0, False)
+            by_second_input(c, 1, True)
+
+        def gains(c0, c1):
+            for c in (c0, c1):
+                nc.scalar.activation(out=pos[c][:], in_=d_ps[c][:], func=ACT.Relu)
+            for c in (c0, c1):
+                nc.scalar.activation(out=root[c][:], in_=pos[c][:], func=ACT.Abs_reciprocal_sqrt, bias=1.0)
+            for c in (c0, c1):
+                nc.scalar.activation(out=gain[c][:], in_=root[c][:], func=ACT.Square)
+
+        def quotient(c):
+            nc.vector.tensor_tensor(out=quot[c][:], in0=p_ps[c][:], in1=gain[c][:], op=ALU.mult)
+
+        def finish(c):
+            for r in range(PACK):
+                cols = slice(CH * r, CH * (r + 1))
+                nc.vector.scalar_tensor_tensor(
+                    out=y[c][:, r, :], in0=d_ps[c][:, cols], scalar=share[:, r : r + 1], in1=quot[c][:, cols],
+                    op0=ALU.mult, op1=ALU.add,
+                )
+            nc.sync.dma_start(
+                out=out_0.rearrange("(p r) t -> p r t", r=PACK)[:, :, CH * c : CH * (c + 1)], in_=y[c][:]
+            )
+
+        def quantize_xq(i):
+            quantize(xq_c[i][:], xq_sc[i][:], xq_bf[i][:])
+
+        def round_xq(engine, i):
+            interleave(engine, xq_bf[i][:], xq_raw[i][:])
+
+        def round_y(engine, c):
+            interleave(engine, y_bf[c][:], y[c][:])
+
+        def quantize_y(c):
+            quantize(y_c[:, CH * c : CH * (c + 1)], y_sc[:, CH * c : CH * (c + 1)], y_bf[c][:])
+
+        def store_words(queue, t0, t1):
+            words = out_1[0].rearrange("p c r -> p (c r)").bitcast(I32)
+            queue.dma_start(out=words[:, t0:t1], in_=y_c[:, t0:t1].bitcast(I32))
+
+        ctx.enter_context(tc.manual_schedule())
+
+        nc.gpsimd.memset(wq_sc_raw[:].bitcast(I32), 0)
+        load_scales(nc.gpsimd, wq_sc_raw, wq_scales)
+        nc.gpsimd.dma_start(out=share[:], in_=sh.rearrange("(p r) o -> p (r o)", r=PACK))
+        nc.vector.memset(xt_sc[:].bitcast(I32), 0)
+        nc.vector.memset(warm_in[:], 1.0)
+        nc.vector.memset(wa_sc_raw[:].bitcast(I32), 0)
+        nc.scalar.activation(out=warm_out[:], in_=warm_in[:], func=ACT.Abs_reciprocal_sqrt)
+
+        nc.sync.dma_start(out=wq_raw[:].bitcast(I32), in_=wq_words.rearrange("z p b -> p z b").bitcast(I32))
+        load_wd(0)
+        load_scales(nc.sync, xt_sc, xt_scales)
+        nc.sync.dma_start(out=xt[:].bitcast(I32), in_=xt_words.rearrange("z p b -> p z b").bitcast(I32))
+        load_wd(1)
+        load_wd(2)
+        nc.sync.dma_start(out=wa_raw[:], in_=wa_words.rearrange("z p n t -> p z (n t)").bitcast(I32))
+        load_scales(nc.sync, wa_sc_raw, wa_scales)
+        for i in range(len(xq_pieces)):
+            load_xq(i)
+
+        deal_wq(0)
+        deal_wq(1)
+
+        round_wd("vector", 0, 0, 84)
+        round_wd("scalar", 0, 84, 128)
+        quantize(wd_c[0][:], wd_sc[0][:], wd_bf[0][:])
+        for c in range(CHUNKS):
+            by_tokens(d_ps[c], c, 0, wd_c[0], wd_sc[0], True, False)
+        round_wd("vector", 1, 0, 32)
+        round_wd("scalar", 1, 32, 64)
+        round_wd("vector", 2, 0, 44)
+        round_wd("scalar", 2, 44, 64)
+        for r in range(PACK):
+            quantize(wd_c[1][:, P * r : P * (r + 1)], wd_sc[1][:, P * r : P * (r + 1)], wd_bf[1][:, 512 * r : 512 * (r + 1)])
+        for c in range(CHUNKS):
+            by_tokens(d_ps[c], c, 1, wd_c[1], wd_sc[1], False, True)
+
+        gains(0, 1)
+        deal_scales(wq_sc, wq_sc_raw)
+        deal_wa(0)
+        deal_wa(1)
+        round_xq("vector", 0)
+        deal_scales(wa_sc, wa_sc_raw)
+        quantize_xq(0)
+        round_xq("vector", 1)
+        quantize_xq(1)
+        sum_products(0)
+        sum_products(1)
+        round_xq("scalar", 2)
+        gains(2, 3)
+        quotient(0)
+        round_xq("vector", 3)
+        finish(0)
+        quantize_xq(2)
+        quantize_xq(3)
+        sum_products(2)
+        quotient(1)
+        round_xq("vector", 4)
+        finish(1)
+        quantize_xq(4)
+        sum_products(3)
+        round_y("scalar", 0)
+        round_y("scalar", 1)
+        quotient(2)
+        quantize_y(0)
+        finish(2)
+        round_y("scalar", 2)
+        quotient(3)
+        quantize_y(1)
+        finish(3)
+        quantize_y(2)
+        store_words(nc.sync, 0, 3 * CH)
+        round_y("vector", 3)
+        quantize_y(3)
+        store_words(nc.scalar, 3 * CH, T)
+        for q in range(4):
+            queue = nc.sync if q % 2 == 0 else nc.scalar
+            queue.dma_start(
+                out=out_2[0, 4 * q : 4 * q + 4, :].bitcast(I32), in_=y_sc[32 * q : 32 * q + 4, :].bitcast(I32)
+            )

@@ -47,13 +47,13 @@ def tile_mix_sum_divided_by_drive_pl_kernel(
         warm_in = tile("warm_in", [P, 1], F32)
         warm_out = tile("warm_out", [P, 1], F32)
 
-        wd_pieces = [(0, 0, N), (1, 0, N // 2), (1, N // 2, N // 2)]
+        wd_pieces = [(0, 0, N), (1, 0, N)]
         wd_raw = [tile("wd_raw%d" % i, [P, PACK, w], F32) for i, (z, n0, w) in enumerate(wd_pieces)]
         wd_bf = [tile("wd_bf%d" % z, [P, PACK * N], BF16) for z in range(PASSES)]
         wd_c = [tile("wd_c%d" % z, [P, N], U32) for z in range(PASSES)]
         wd_sc = [tile("wd_sc%d" % z, [P, N], U8) for z in range(PASSES)]
 
-        xq_pieces = [(0, 0, 256), (1, 0, 256), (0, 256, 256), (1, 256, 128), (1, 384, 128)]
+        xq_pieces = [(z, CH * c, CH) for c in range(CHUNKS) for z in range(PASSES)]
         xq_raw = [tile("xq_raw%d" % i, [P, PACK, w], F32) for i, (z, t0, w) in enumerate(xq_pieces)]
         xq_bf = [tile("xq_bf%d" % i, [P, PACK * w], BF16) for i, (z, t0, w) in enumerate(xq_pieces)]
         xq_c = [tile("xq_c%d" % i, [P, w], U32) for i, (z, t0, w) in enumerate(xq_pieces)]
@@ -71,8 +71,8 @@ def tile_mix_sum_divided_by_drive_pl_kernel(
         d_ps = [ps.tile([P, PACK * CH], F32, name="d_ps%d" % c) for c in range(CHUNKS)]
         p_ps = [ps.tile([P, PACK * CH], F32, name="p_ps%d" % c) for c in range(CHUNKS)]
 
-        def load_scales(queue, plane, scales):
-            for q in range(4):
+        def load_scales(queue, plane, scales, quadrants=range(4)):
+            for q in quadrants:
                 queue.dma_start(
                     out=plane[32 * q : 32 * q + 4, :, :].bitcast(I32),
                     in_=scales[:, 4 * q : 4 * q + 4, :].rearrange("z r c -> r z c").bitcast(I32),
@@ -140,7 +140,7 @@ def tile_mix_sum_divided_by_drive_pl_kernel(
                     stop=(stop and r == PACK - 1),
                 )
 
-        def by_second_input(c, z, stop):
+        def by_second_input(c, z, start, stop):
             i = [k for k, (zz, t0, w) in enumerate(xq_pieces) if zz == z and t0 <= CH * c < t0 + w][0]
             t = CH * c - xq_pieces[i][1]
             for r in range(PACK):
@@ -150,15 +150,13 @@ def tile_mix_sum_divided_by_drive_pl_kernel(
                     lhsT_scale=wq_sc[:, z, P * r : P * (r + 1)],
                     rhs=xq_c[i][:, t : t + CH].bitcast(FP8X4),
                     rhs_scale=xq_sc[i][:, t : t + CH],
-                    start=False,
+                    start=(start and r == 0),
                     stop=(stop and r == PACK - 1),
                 )
 
-        def sum_products(c):
+        def first_product(c):
             by_tokens(p_ps[c], c, 0, wa[0], wa_sc[:, 0, :], True, False)
             by_tokens(p_ps[c], c, 1, wa[1], wa_sc[:, 1, :], False, False)
-            by_second_input(c, 0, False)
-            by_second_input(c, 1, True)
 
         def gains(c0, c1):
             for c in (c0, c1):
@@ -168,16 +166,23 @@ def tile_mix_sum_divided_by_drive_pl_kernel(
             for c in (c0, c1):
                 nc.scalar.activation(out=gain[c][:], in_=root[c][:], func=ACT.Square)
 
-        def quotient(c):
-            nc.vector.tensor_tensor(out=quot[c][:], in0=p_ps[c][:], in1=gain[c][:], op=ALU.mult)
+        def quotient(c, r):
+            cols = slice(CH * r, CH * (r + 1))
+            nc.vector.tensor_tensor(out=quot[c][:, cols], in0=p_ps[c][:, cols], in1=gain[c][:, cols], op=ALU.mult)
+
+        def add_share(c, r):
+            cols = slice(CH * r, CH * (r + 1))
+            nc.vector.scalar_tensor_tensor(
+                out=y[c][:, r, :], in0=d_ps[c][:, cols], scalar=share[:, r : r + 1], in1=quot[c][:, cols],
+                op0=ALU.mult, op1=ALU.add,
+            )
 
         def finish(c):
-            for r in range(PACK):
-                cols = slice(CH * r, CH * (r + 1))
-                nc.vector.scalar_tensor_tensor(
-                    out=y[c][:, r, :], in0=d_ps[c][:, cols], scalar=share[:, r : r + 1], in1=quot[c][:, cols],
-                    op0=ALU.mult, op1=ALU.add,
-                )
+            for step in range(PACK + 2):
+                if step < PACK:
+                    quotient(c, step)
+                if step >= 2:
+                    add_share(c, step - 2)
             nc.sync.dma_start(
                 out=out_0.rearrange("(p r) t -> p r t", r=PACK)[:, :, CH * c : CH * (c + 1)], in_=y[c][:]
             )
@@ -200,80 +205,116 @@ def tile_mix_sum_divided_by_drive_pl_kernel(
 
         ctx.enter_context(tc.manual_schedule())
 
-        nc.gpsimd.memset(wq_sc_raw[:].bitcast(I32), 0)
-        load_scales(nc.gpsimd, wq_sc_raw, wq_scales)
-        nc.gpsimd.dma_start(out=share[:], in_=sh.rearrange("(p r) o -> p (r o)", r=PACK))
         nc.vector.memset(xt_sc[:].bitcast(I32), 0)
         nc.vector.memset(warm_in[:], 1.0)
-        nc.vector.memset(wa_sc_raw[:].bitcast(I32), 0)
         nc.scalar.activation(out=warm_out[:], in_=warm_in[:], func=ACT.Abs_reciprocal_sqrt)
-
-        nc.sync.dma_start(out=wq_raw[:].bitcast(I32), in_=wq_words.rearrange("z p b -> p z b").bitcast(I32))
+        nc.vector.memset(wa_sc_raw[:].bitcast(I32), 0)
+        nc.vector.memset(wq_sc_raw[:].bitcast(I32), 0)
         load_wd(0)
-        load_scales(nc.sync, xt_sc, xt_scales)
-        nc.sync.dma_start(out=xt[:].bitcast(I32), in_=xt_words.rearrange("z p b -> p z b").bitcast(I32))
+        load_scales(nc.sync, xt_sc, xt_scales, (0,))
+        load_scales(nc.sync, xt_sc, xt_scales, (1,))
+        load_scales(nc.sync, xt_sc, xt_scales, (2,))
+        load_scales(nc.sync, xt_sc, xt_scales, (3,))
         load_wd(1)
-        load_wd(2)
+        nc.sync.dma_start(out=xt[:].bitcast(I32), in_=xt_words.rearrange("z p b -> p z b").bitcast(I32))
         nc.sync.dma_start(out=wa_raw[:], in_=wa_words.rearrange("z p n t -> p z (n t)").bitcast(I32))
-        load_scales(nc.sync, wa_sc_raw, wa_scales)
-        for i in range(len(xq_pieces)):
-            load_xq(i)
-
-        deal_wq(0)
-        deal_wq(1)
-
-        round_wd("vector", 0, 0, 84)
-        round_wd("scalar", 0, 84, 128)
+        load_scales(nc.sync, wa_sc_raw, wa_scales, (0,))
+        load_scales(nc.sync, wa_sc_raw, wa_scales, (1,))
+        load_scales(nc.sync, wa_sc_raw, wa_scales, (2,))
+        load_scales(nc.sync, wa_sc_raw, wa_scales, (3,))
+        nc.sync.dma_start(out=wq_raw[:].bitcast(I32), in_=wq_words.rearrange("z p b -> p z b").bitcast(I32))
+        load_xq(0)
+        load_scales(nc.sync, wq_sc_raw, wq_scales, (0,))
+        load_scales(nc.sync, wq_sc_raw, wq_scales, (1,))
+        load_scales(nc.sync, wq_sc_raw, wq_scales, (2,))
+        load_scales(nc.sync, wq_sc_raw, wq_scales, (3,))
+        load_xq(1)
+        load_xq(2)
+        load_xq(3)
+        nc.sync.dma_start(out=share[:], in_=sh.rearrange("(p r) o -> p (r o)", r=PACK))
+        load_xq(4)
+        load_xq(5)
+        load_xq(6)
+        load_xq(7)
+        round_wd("vector", 0, 0, 92)
+        round_wd("scalar", 0, 92, wd_pieces[0][2] // PACK)
         quantize(wd_c[0][:], wd_sc[0][:], wd_bf[0][:])
-        for c in range(CHUNKS):
-            by_tokens(d_ps[c], c, 0, wd_c[0], wd_sc[0], True, False)
-        round_wd("vector", 1, 0, 32)
-        round_wd("scalar", 1, 32, 64)
-        round_wd("vector", 2, 0, 44)
-        round_wd("scalar", 2, 44, 64)
+        by_tokens(d_ps[0], 0, 0, wd_c[0], wd_sc[0], True, False)
+        by_tokens(d_ps[1], 1, 0, wd_c[0], wd_sc[0], True, False)
+        round_wd("vector", 1, 0, 92)
+        round_wd("scalar", 1, 92, wd_pieces[1][2] // PACK)
         for r in range(PACK):
             quantize(wd_c[1][:, P * r : P * (r + 1)], wd_sc[1][:, P * r : P * (r + 1)], wd_bf[1][:, 512 * r : 512 * (r + 1)])
-        for c in range(CHUNKS):
-            by_tokens(d_ps[c], c, 1, wd_c[1], wd_sc[1], False, True)
-
-        gains(0, 1)
-        deal_scales(wq_sc, wq_sc_raw)
+        by_tokens(d_ps[0], 0, 1, wd_c[1], wd_sc[1], False, True)
+        by_tokens(d_ps[1], 1, 1, wd_c[1], wd_sc[1], False, True)
+        by_tokens(d_ps[2], 2, 0, wd_c[0], wd_sc[0], True, False)
+        by_tokens(d_ps[2], 2, 1, wd_c[1], wd_sc[1], False, True)
+        by_tokens(d_ps[3], 3, 0, wd_c[0], wd_sc[0], True, False)
+        by_tokens(d_ps[3], 3, 1, wd_c[1], wd_sc[1], False, True)
+        nc.scalar.activation(out=pos[0][:], in_=d_ps[0][:], func=ACT.Relu)
+        nc.scalar.activation(out=pos[1][:], in_=d_ps[1][:], func=ACT.Relu)
+        nc.scalar.activation(out=root[0][:], in_=pos[0][:], func=ACT.Abs_reciprocal_sqrt, bias=1.0)
+        nc.scalar.activation(out=root[1][:], in_=pos[1][:], func=ACT.Abs_reciprocal_sqrt, bias=1.0)
+        nc.scalar.activation(out=gain[0][:], in_=root[0][:], func=ACT.Square)
+        nc.scalar.activation(out=gain[1][:], in_=root[1][:], func=ACT.Square)
+        nc.scalar.activation(out=pos[2][:], in_=d_ps[2][:], func=ACT.Relu)
+        nc.scalar.activation(out=pos[3][:], in_=d_ps[3][:], func=ACT.Relu)
+        nc.scalar.activation(out=root[2][:], in_=pos[2][:], func=ACT.Abs_reciprocal_sqrt, bias=1.0)
         deal_wa(0)
         deal_wa(1)
-        round_xq("vector", 0)
         deal_scales(wa_sc, wa_sc_raw)
+        by_tokens(p_ps[0], 0, 0, wa[0], wa_sc[:, 0, :], True, False)
+        by_tokens(p_ps[0], 0, 1, wa[1], wa_sc[:, 1, :], False, False)
+        by_tokens(p_ps[1], 1, 0, wa[0], wa_sc[:, 0, :], True, False)
+        by_tokens(p_ps[1], 1, 1, wa[1], wa_sc[:, 1, :], False, False)
+        by_tokens(p_ps[2], 2, 0, wa[0], wa_sc[:, 0, :], True, False)
+        by_tokens(p_ps[2], 2, 1, wa[1], wa_sc[:, 1, :], False, False)
+        deal_wq(0)
+        deal_wq(1)
+        round_xq("vector", 0)
+        deal_scales(wq_sc, wq_sc_raw)
         quantize_xq(0)
+        by_second_input(0, 0, False, False)
         round_xq("vector", 1)
         quantize_xq(1)
-        sum_products(0)
-        sum_products(1)
-        round_xq("scalar", 2)
-        gains(2, 3)
-        quotient(0)
+        by_second_input(0, 1, False, True)
+        by_tokens(p_ps[3], 3, 0, wa[0], wa_sc[:, 0, :], True, False)
+        by_tokens(p_ps[3], 3, 1, wa[1], wa_sc[:, 1, :], False, False)
+        round_xq("vector", 2)
         round_xq("vector", 3)
-        finish(0)
         quantize_xq(2)
         quantize_xq(3)
-        sum_products(2)
-        quotient(1)
-        round_xq("vector", 4)
-        finish(1)
+        by_second_input(1, 0, False, False)
+        by_second_input(1, 1, False, True)
+        round_xq("scalar", 4)
+        finish(0)
+        round_xq("vector", 5)
         quantize_xq(4)
-        sum_products(3)
+        quantize_xq(5)
+        by_second_input(2, 0, False, False)
+        by_second_input(2, 1, False, True)
+        nc.scalar.activation(out=gain[2][:], in_=root[2][:], func=ACT.Square)
+        nc.scalar.activation(out=root[3][:], in_=pos[3][:], func=ACT.Abs_reciprocal_sqrt, bias=1.0)
+        round_xq("scalar", 6)
+        finish(1)
+        round_xq("vector", 7)
+        quantize_xq(6)
+        quantize_xq(7)
+        by_second_input(3, 0, False, False)
+        by_second_input(3, 1, False, True)
+        nc.scalar.activation(out=gain[3][:], in_=root[3][:], func=ACT.Square)
         round_y("scalar", 0)
         round_y("scalar", 1)
-        quotient(2)
-        quantize_y(0)
         finish(2)
         round_y("scalar", 2)
-        quotient(3)
+        quantize_y(0)
         quantize_y(1)
+        store_words(nc.sync, 0 * CH, 2 * CH)
         finish(3)
         quantize_y(2)
-        store_words(nc.sync, 0, 3 * CH)
         round_y("vector", 3)
         quantize_y(3)
-        store_words(nc.scalar, 3 * CH, T)
+        store_words(nc.scalar, 2 * CH, 4 * CH)
         for q in range(4):
             queue = nc.sync if q % 2 == 0 else nc.scalar
             queue.dma_start(

@@ -96,9 +96,9 @@ def tile_mix_sum_divided_by_drive_pl_kernel(
 
         def round_wd(engine, i, m0, m1):
             z, n0, w = wd_pieces[i]
-            src = wd_raw[i][:].rearrange("p j (m r) -> p m j r", r=PACK)[:, m0:m1, :, :]
-            dst = wd_bf[z][:].rearrange("p (r m j) -> p m j r", r=PACK, j=PACK)
-            copy_on(engine, dst[:, n0 // PACK + m0 : n0 // PACK + m1, :, :], src)
+            src = wd_raw[i][:].rearrange("p (h e) (m r) -> p m h r e", e=2, r=PACK)[:, m0:m1]
+            dst = wd_bf[z][:].rearrange("p (r m h e) -> p m h r e", r=PACK, h=2, e=2)
+            copy_on(engine, dst[:, n0 // PACK + m0 : n0 // PACK + m1], src)
 
         def interleave(engine, dst, src):
             copy_on(
@@ -177,12 +177,23 @@ def tile_mix_sum_divided_by_drive_pl_kernel(
                 op0=ALU.mult, op1=ALU.add,
             )
 
-        def finish(c):
+        def quotients(c):
+            nc.vector.tensor_tensor(out=quot[c][:], in0=p_ps[c][:], in1=gain[c][:], op=ALU.mult)
+
+        def finish_by_rows(c):
             for step in range(PACK + 2):
                 if step < PACK:
                     quotient(c, step)
                 if step >= 2:
                     add_share(c, step - 2)
+            store_y(c)
+
+        def finish(c):
+            for r in range(PACK):
+                add_share(c, r)
+            store_y(c)
+
+        def store_y(c):
             nc.sync.dma_start(
                 out=out_0.rearrange("(p r) t -> p r t", r=PACK)[:, :, CH * c : CH * (c + 1)], in_=y[c][:]
             )
@@ -194,7 +205,13 @@ def tile_mix_sum_divided_by_drive_pl_kernel(
             interleave(engine, xq_bf[i][:], xq_raw[i][:])
 
         def round_y(engine, c):
-            interleave(engine, y_bf[c][:], y[c][:])
+            if engine == "gpsimd":
+                nc.gpsimd.tensor_scalar(
+                    out=y_bf[c][:].rearrange("p (t r) -> p t r", r=PACK), in0=y[c][:].rearrange("p r t -> p t r"),
+                    scalar1=1.0, scalar2=-0.0, op0=ALU.mult, op1=ALU.add,
+                )
+            else:
+                interleave(engine, y_bf[c][:], y[c][:])
 
         def quantize_y(c):
             quantize(y_c[:, CH * c : CH * (c + 1)], y_sc[:, CH * c : CH * (c + 1)], y_bf[c][:])
@@ -205,11 +222,16 @@ def tile_mix_sum_divided_by_drive_pl_kernel(
 
         ctx.enter_context(tc.manual_schedule())
 
+        nc.gpsimd.memset(wq_sc_raw[:].bitcast(I32), 0)
+        load_scales(nc.gpsimd, wq_sc_raw, wq_scales, (0,))
+        load_scales(nc.gpsimd, wq_sc_raw, wq_scales, (1,))
+        load_scales(nc.gpsimd, wq_sc_raw, wq_scales, (2,))
+        load_scales(nc.gpsimd, wq_sc_raw, wq_scales, (3,))
+        nc.gpsimd.dma_start(out=share[:], in_=sh.rearrange("(p r) o -> p (r o)", r=PACK))
         nc.vector.memset(xt_sc[:].bitcast(I32), 0)
         nc.vector.memset(warm_in[:], 1.0)
         nc.scalar.activation(out=warm_out[:], in_=warm_in[:], func=ACT.Abs_reciprocal_sqrt)
         nc.vector.memset(wa_sc_raw[:].bitcast(I32), 0)
-        nc.vector.memset(wq_sc_raw[:].bitcast(I32), 0)
         load_wd(0)
         load_scales(nc.sync, xt_sc, xt_scales, (0,))
         load_scales(nc.sync, xt_sc, xt_scales, (1,))
@@ -224,14 +246,9 @@ def tile_mix_sum_divided_by_drive_pl_kernel(
         load_scales(nc.sync, wa_sc_raw, wa_scales, (3,))
         nc.sync.dma_start(out=wq_raw[:].bitcast(I32), in_=wq_words.rearrange("z p b -> p z b").bitcast(I32))
         load_xq(0)
-        load_scales(nc.sync, wq_sc_raw, wq_scales, (0,))
-        load_scales(nc.sync, wq_sc_raw, wq_scales, (1,))
-        load_scales(nc.sync, wq_sc_raw, wq_scales, (2,))
-        load_scales(nc.sync, wq_sc_raw, wq_scales, (3,))
         load_xq(1)
         load_xq(2)
         load_xq(3)
-        nc.sync.dma_start(out=share[:], in_=sh.rearrange("(p r) o -> p (r o)", r=PACK))
         load_xq(4)
         load_xq(5)
         load_xq(6)
@@ -257,9 +274,7 @@ def tile_mix_sum_divided_by_drive_pl_kernel(
         nc.scalar.activation(out=root[1][:], in_=pos[1][:], func=ACT.Abs_reciprocal_sqrt, bias=1.0)
         nc.scalar.activation(out=gain[0][:], in_=root[0][:], func=ACT.Square)
         nc.scalar.activation(out=gain[1][:], in_=root[1][:], func=ACT.Square)
-        nc.scalar.activation(out=pos[2][:], in_=d_ps[2][:], func=ACT.Relu)
-        nc.scalar.activation(out=pos[3][:], in_=d_ps[3][:], func=ACT.Relu)
-        nc.scalar.activation(out=root[2][:], in_=pos[2][:], func=ACT.Abs_reciprocal_sqrt, bias=1.0)
+        deal_scales(wq_sc, wq_sc_raw)
         deal_wa(0)
         deal_wa(1)
         deal_scales(wa_sc, wa_sc_raw)
@@ -267,54 +282,60 @@ def tile_mix_sum_divided_by_drive_pl_kernel(
         by_tokens(p_ps[0], 0, 1, wa[1], wa_sc[:, 1, :], False, False)
         by_tokens(p_ps[1], 1, 0, wa[0], wa_sc[:, 0, :], True, False)
         by_tokens(p_ps[1], 1, 1, wa[1], wa_sc[:, 1, :], False, False)
-        by_tokens(p_ps[2], 2, 0, wa[0], wa_sc[:, 0, :], True, False)
-        by_tokens(p_ps[2], 2, 1, wa[1], wa_sc[:, 1, :], False, False)
         deal_wq(0)
         deal_wq(1)
         round_xq("vector", 0)
-        deal_scales(wq_sc, wq_sc_raw)
         quantize_xq(0)
         by_second_input(0, 0, False, False)
         round_xq("vector", 1)
         quantize_xq(1)
         by_second_input(0, 1, False, True)
-        by_tokens(p_ps[3], 3, 0, wa[0], wa_sc[:, 0, :], True, False)
-        by_tokens(p_ps[3], 3, 1, wa[1], wa_sc[:, 1, :], False, False)
+        by_tokens(p_ps[2], 2, 0, wa[0], wa_sc[:, 0, :], True, False)
+        by_tokens(p_ps[2], 2, 1, wa[1], wa_sc[:, 1, :], False, False)
         round_xq("vector", 2)
+        nc.scalar.activation(out=pos[2][:], in_=d_ps[2][:], func=ACT.Relu)
+        nc.scalar.activation(out=pos[3][:], in_=d_ps[3][:], func=ACT.Relu)
+        nc.scalar.activation(out=root[2][:], in_=pos[2][:], func=ACT.Abs_reciprocal_sqrt, bias=1.0)
         round_xq("vector", 3)
         quantize_xq(2)
-        quantize_xq(3)
         by_second_input(1, 0, False, False)
+        quotients(0)
+        quantize_xq(3)
         by_second_input(1, 1, False, True)
+        by_tokens(p_ps[3], 3, 0, wa[0], wa_sc[:, 0, :], True, False)
+        by_tokens(p_ps[3], 3, 1, wa[1], wa_sc[:, 1, :], False, False)
         round_xq("scalar", 4)
         finish(0)
         round_xq("vector", 5)
         quantize_xq(4)
-        quantize_xq(5)
         by_second_input(2, 0, False, False)
-        by_second_input(2, 1, False, True)
         nc.scalar.activation(out=gain[2][:], in_=root[2][:], func=ACT.Square)
         nc.scalar.activation(out=root[3][:], in_=pos[3][:], func=ACT.Abs_reciprocal_sqrt, bias=1.0)
+        quotients(1)
+        quantize_xq(5)
+        by_second_input(2, 1, False, True)
         round_xq("scalar", 6)
         finish(1)
         round_xq("vector", 7)
         quantize_xq(6)
-        quantize_xq(7)
         by_second_input(3, 0, False, False)
-        by_second_input(3, 1, False, True)
         nc.scalar.activation(out=gain[3][:], in_=root[3][:], func=ACT.Square)
         round_y("scalar", 0)
         round_y("scalar", 1)
+        quotients(2)
+        quantize_xq(7)
+        by_second_input(3, 1, False, True)
+        quantize_y(0)
         finish(2)
         round_y("scalar", 2)
-        quantize_y(0)
         quantize_y(1)
         store_words(nc.sync, 0 * CH, 2 * CH)
-        finish(3)
+        finish_by_rows(3)
         quantize_y(2)
+        store_words(nc.sync, 2 * CH, 3 * CH)
         round_y("vector", 3)
         quantize_y(3)
-        store_words(nc.scalar, 2 * CH, 4 * CH)
+        store_words(nc.scalar, 3 * CH, 4 * CH)
         for q in range(4):
             queue = nc.sync if q % 2 == 0 else nc.scalar
             queue.dma_start(

@@ -2,7 +2,7 @@ from contextlib import ExitStack
 
 import concourse.mybir as mybir
 
-K, L, T, N = 1024, 1024, 512, 512
+K, T, N = 1024, 512, 512
 FLOPS = 3 * 2 * K * N * T
 
 F32 = mybir.dt.float32
@@ -17,9 +17,14 @@ ACT = mybir.ActivationFunctionType
 
 P = 128
 PACK = 4
-PASSES = 2
+K_PASS = P * PACK
+PASSES = K // K_PASS
+QUADRANTS = 4
 CH = 128
 CHUNKS = T // CH
+LINE = 16
+WD_ON_VECTOR = 92
+FIRST_LATE_CHUNK = 2
 
 
 def tile_mix_sum_divided_by_drive_pl_kernel(
@@ -27,317 +32,242 @@ def tile_mix_sum_divided_by_drive_pl_kernel(
 ):
     nc = tc.nc
     with ExitStack() as ctx:
-        sb = ctx.enter_context(tc.tile_pool(name="sb", bufs=1))
-        ps = ctx.enter_context(tc.psum_pool(name="ps", bufs=1))
+        sbuf = ctx.enter_context(tc.tile_pool(name="sbuf", bufs=1))
+        psum = ctx.enter_context(tc.psum_pool(name="psum", bufs=1))
 
         def tile(name, shape, dtype):
-            return sb.tile(shape, dtype, name=name, align_bytes=64)
+            return sbuf.tile(shape, dtype, name=name, align_bytes=64)
+
+        def by_pass(name, shape, dtype):
+            return [tile("%s%d" % (name, z), shape, dtype) for z in range(PASSES)]
+
+        def by_chunk(name, shape, dtype):
+            return [tile("%s%d" % (name, c), shape, dtype) for c in range(CHUNKS)]
 
         xt = tile("xt", [P, PASSES, 2 * T], U8)
-        xt_sc = tile("xt_sc", [P, PASSES, T], U8)
+        xt_plane = tile("xt_plane", [P, PASSES, T], U8)
         wq_raw = tile("wq_raw", [P, PASSES, 2 * N], U8)
-        wq_sc_raw = tile("wq_sc_raw", [P, PASSES, N], U8)
+        wq_plane_raw = tile("wq_plane_raw", [P, PASSES, N], U8)
         wa_raw = tile("wa_raw", [P, PASSES, N], I32)
-        wa_sc_raw = tile("wa_sc_raw", [P, PASSES, N], U8)
-        wq = [tile("wq%d" % z, [P, 2 * N], U8) for z in range(PASSES)]
-        wa = [tile("wa%d" % z, [P, N], U32) for z in range(PASSES)]
-        wq_sc = tile("wq_sc", [P, PASSES, N], U8)
-        wa_sc = tile("wa_sc", [P, PASSES, N], U8)
+        wa_plane_raw = tile("wa_plane_raw", [P, PASSES, N], U8)
+        wq = by_pass("wq", [P, 2 * N], U8)
+        wa = by_pass("wa", [P, N], U32)
+        wq_plane = tile("wq_plane", [P, PASSES, N], U8)
+        wa_plane = tile("wa_plane", [P, PASSES, N], U8)
         share = tile("share", [P, PACK], F32)
-        warm_in = tile("warm_in", [P, 1], F32)
-        warm_out = tile("warm_out", [P, 1], F32)
+        table_in = tile("table_in", [P, 1], F32)
+        table_out = tile("table_out", [P, 1], F32)
 
-        wd_pieces = [(0, 0, N), (1, 0, N)]
-        wd_raw = [tile("wd_raw%d" % i, [P, PACK, w], F32) for i, (z, n0, w) in enumerate(wd_pieces)]
-        wd_bf = [tile("wd_bf%d" % z, [P, PACK * N], BF16) for z in range(PASSES)]
-        wd_c = [tile("wd_c%d" % z, [P, N], U32) for z in range(PASSES)]
-        wd_sc = [tile("wd_sc%d" % z, [P, N], U8) for z in range(PASSES)]
+        wd_raw = by_pass("wd_raw", [P, PACK, N], F32)
+        wd_bf = by_pass("wd_bf", [P, PACK * N], BF16)
+        wd_codes = by_pass("wd_codes", [P, N], U32)
+        wd_plane = by_pass("wd_plane", [P, N], U8)
+        xq_raw = [by_pass("xq_raw%d_" % c, [P, PACK, CH], F32) for c in range(CHUNKS)]
+        xq_bf = [by_pass("xq_bf%d_" % c, [P, PACK * CH], BF16) for c in range(CHUNKS)]
+        xq_codes = [by_pass("xq_codes%d_" % c, [P, CH], U32) for c in range(CHUNKS)]
+        xq_plane = [by_pass("xq_plane%d_" % c, [P, CH], U8) for c in range(CHUNKS)]
 
-        xq_pieces = [(z, CH * c, CH) for c in range(CHUNKS) for z in range(PASSES)]
-        xq_raw = [tile("xq_raw%d" % i, [P, PACK, w], F32) for i, (z, t0, w) in enumerate(xq_pieces)]
-        xq_bf = [tile("xq_bf%d" % i, [P, PACK * w], BF16) for i, (z, t0, w) in enumerate(xq_pieces)]
-        xq_c = [tile("xq_c%d" % i, [P, w], U32) for i, (z, t0, w) in enumerate(xq_pieces)]
-        xq_sc = [tile("xq_sc%d" % i, [P, w], U8) for i, (z, t0, w) in enumerate(xq_pieces)]
+        positive = by_chunk("positive", [P, PACK * CH], F32)
+        root = by_chunk("root", [P, PACK * CH], F32)
+        gain = by_chunk("gain", [P, PACK * CH], F32)
+        quotient = by_chunk("quotient", [P, PACK * CH], F32)
+        y = by_chunk("y", [P, PACK, CH], F32)
+        y_bf = by_chunk("y_bf", [P, PACK * CH], BF16)
+        y_codes = tile("y_codes", [P, T], U32)
+        y_plane = tile("y_plane", [P, T], U8)
 
-        pos = [tile("pos%d" % c, [P, PACK * CH], F32) for c in range(CHUNKS)]
-        root = [tile("root%d" % c, [P, PACK * CH], F32) for c in range(CHUNKS)]
-        gain = [tile("gain%d" % c, [P, PACK * CH], F32) for c in range(CHUNKS)]
-        quot = [tile("quot%d" % c, [P, PACK * CH], F32) for c in range(CHUNKS)]
-        y = [tile("y%d" % c, [P, PACK, CH], F32) for c in range(CHUNKS)]
-        y_bf = [tile("y_bf%d" % c, [P, PACK * CH], BF16) for c in range(CHUNKS)]
-        y_c = tile("y_c", [P, T], U32)
-        y_sc = tile("y_sc", [P, T], U8)
+        d_bank = [psum.tile([P, PACK * CH], F32, name="d_bank%d" % c) for c in range(CHUNKS)]
+        p_bank = [psum.tile([P, PACK * CH], F32, name="p_bank%d" % c) for c in range(CHUNKS)]
 
-        d_ps = [ps.tile([P, PACK * CH], F32, name="d_ps%d" % c) for c in range(CHUNKS)]
-        p_ps = [ps.tile([P, PACK * CH], F32, name="p_ps%d" % c) for c in range(CHUNKS)]
+        def span(i, width):
+            return slice(width * i, width * (i + 1))
 
-        def load_scales(queue, plane, scales, quadrants=range(4)):
-            for q in quadrants:
-                queue.dma_start(
+        def load_scales(plane, scales):
+            for q in range(QUADRANTS):
+                nc.sync.dma_start(
                     out=plane[32 * q : 32 * q + 4, :, :].bitcast(I32),
-                    in_=scales[:, 4 * q : 4 * q + 4, :].rearrange("z r c -> r z c").bitcast(I32),
+                    in_=scales[:, span(q, 4), :].rearrange("z r c -> r z c").bitcast(I32),
                 )
 
-        def load_wd(i):
-            z, n0, w = wd_pieces[i]
-            rows = wd[512 * z : 512 * (z + 1), :].rearrange("(p j) n -> p j n", j=PACK)
-            nc.sync.dma_start(out=wd_raw[i][:], in_=rows[:, :, n0 : n0 + w])
+        def load_rows(raw, matrix, z, cols):
+            rows = matrix[span(z, K_PASS), :].rearrange("(p j) c -> p j c", j=PACK)
+            nc.sync.dma_start(out=raw[:], in_=rows[:, :, cols])
 
-        def load_xq(i):
-            z, t0, w = xq_pieces[i]
-            rows = xq[512 * z : 512 * (z + 1), :].rearrange("(p j) t -> p j t", j=PACK)
-            nc.sync.dma_start(out=xq_raw[i][:], in_=rows[:, :, t0 : t0 + w])
-
-        def copy_on(engine, out, in_):
-            if engine == "vector":
-                nc.vector.tensor_copy(out=out, in_=in_)
-            else:
-                nc.scalar.copy(out=out, in_=in_)
-
-        def round_wd(engine, i, m0, m1):
-            z, n0, w = wd_pieces[i]
-            src = wd_raw[i][:].rearrange("p (h e) (m r) -> p m h r e", e=2, r=PACK)[:, m0:m1]
-            dst = wd_bf[z][:].rearrange("p (r m h e) -> p m h r e", r=PACK, h=2, e=2)
-            copy_on(engine, dst[:, n0 // PACK + m0 : n0 // PACK + m1], src)
-
-        def interleave(engine, dst, src):
-            copy_on(
-                engine,
-                dst.rearrange("p (c i j) -> p c j i", i=4, j=PACK),
-                src.rearrange("p j (c i) -> p c j i", i=4),
-            )
-
-        def quantize(codes, scales, values):
-            nc.vector.quantize_mx(out=codes.bitcast(FP8X4), scales=scales, in_=values)
-
-        def deal_scales(dst, src):
+        def deal_plane(plane, raw):
             nc.vector.tensor_copy(
-                out=dst[:].rearrange("p z (r a b) -> p z a r b", r=PACK, b=16),
-                in_=src[:].rearrange("p z (a b r) -> p z a r b", r=PACK, b=16),
+                out=plane[:].rearrange("p z (r a b) -> p z a r b", r=PACK, b=LINE),
+                in_=raw[:].rearrange("p z (a b r) -> p z a r b", r=PACK, b=LINE),
             )
 
         def deal_wq(z):
             nc.vector.tensor_copy(
-                out=wq[z][:].rearrange("p (r a b e) -> p a r b e", r=PACK, b=8, e=2),
-                in_=wq_raw[:, z, :].rearrange("p (a b r e) -> p a r b e", r=PACK, b=8, e=2),
+                out=wq[z][:].rearrange("p (r a b e) -> p a r b e", r=PACK, b=LINE // 2, e=2),
+                in_=wq_raw[:, z, :].rearrange("p (a b r e) -> p a r b e", r=PACK, b=LINE // 2, e=2),
             )
 
         def deal_wa(z):
             nc.vector.tensor_copy(
-                out=wa[z][:].bitcast(I32).rearrange("p (r a b) -> p a r b", r=PACK, b=4),
-                in_=wa_raw[:, z, :].rearrange("p (a b r) -> p a r b", r=PACK, b=4),
+                out=wa[z][:].bitcast(I32).rearrange("p (r a b) -> p a r b", r=PACK, b=LINE // 4),
+                in_=wa_raw[:, z, :].rearrange("p (a b r) -> p a r b", r=PACK, b=LINE // 4),
             )
 
-        def by_tokens(bank, c, z, codes, scales, start, stop):
+        def round_wd(z):
+            src = wd_raw[z][:].rearrange("p j (m r) -> p m j r", r=PACK)
+            dst = wd_bf[z][:].rearrange("p (r m j) -> p m j r", r=PACK, j=PACK)
+            nc.vector.tensor_copy(out=dst[:, :WD_ON_VECTOR], in_=src[:, :WD_ON_VECTOR])
+            nc.scalar.copy(out=dst[:, WD_ON_VECTOR:], in_=src[:, WD_ON_VECTOR:])
+
+        def round_rows(copy, dst, src):
+            copy(
+                out=dst[:].rearrange("p (g i j) -> p g j i", i=4, j=PACK),
+                in_=src[:].rearrange("p j (g i) -> p g j i", i=4),
+            )
+
+        def quantize(codes, plane, values):
+            nc.vector.quantize_mx(out=codes.bitcast(FP8X4), scales=plane, in_=values)
+
+        def mx_pass(bank, weights, weights_plane, weights_dtype, moving, moving_plane, start, stop):
+            width = weights.shape[1] // PACK
             for r in range(PACK):
                 nc.tensor.matmul_mx(
-                    out=bank[:, CH * r : CH * (r + 1)],
-                    lhsT=codes[:, P * r : P * (r + 1)].bitcast(FP8X4),
-                    lhsT_scale=scales[:, P * r : P * (r + 1)],
-                    rhs=xt[:, z, 2 * CH * c : 2 * CH * (c + 1)].bitcast(FP4X4),
-                    rhs_scale=xt_sc[:, z, CH * c : CH * (c + 1)],
+                    out=bank[:, span(r, CH)],
+                    lhsT=weights[:, span(r, width)].bitcast(weights_dtype),
+                    lhsT_scale=weights_plane[:, span(r, P)],
+                    rhs=moving,
+                    rhs_scale=moving_plane,
                     start=(start and r == 0),
                     stop=(stop and r == PACK - 1),
                 )
 
-        def by_second_input(c, z, start, stop):
-            i = [k for k, (zz, t0, w) in enumerate(xq_pieces) if zz == z and t0 <= CH * c < t0 + w][0]
-            t = CH * c - xq_pieces[i][1]
-            for r in range(PACK):
-                nc.tensor.matmul_mx(
-                    out=p_ps[c][:, CH * r : CH * (r + 1)],
-                    lhsT=wq[z][:, 2 * P * r : 2 * P * (r + 1)].bitcast(FP4X4),
-                    lhsT_scale=wq_sc[:, z, P * r : P * (r + 1)],
-                    rhs=xq_c[i][:, t : t + CH].bitcast(FP8X4),
-                    rhs_scale=xq_sc[i][:, t : t + CH],
-                    start=(start and r == 0),
-                    stop=(stop and r == PACK - 1),
-                )
+        def tokens_pass(bank, c, z, weights, weights_plane, start, stop):
+            moving = xt[:, z, span(c, 2 * CH)].bitcast(FP4X4)
+            mx_pass(bank, weights, weights_plane, FP8X4, moving, xt_plane[:, z, span(c, CH)], start, stop)
+
+        def drive_passes(chunks, z):
+            for c in chunks:
+                tokens_pass(d_bank[c], c, z, wd_codes[z][:], wd_plane[z][:], z == 0, z == PASSES - 1)
 
         def first_product(c):
-            by_tokens(p_ps[c], c, 0, wa[0], wa_sc[:, 0, :], True, False)
-            by_tokens(p_ps[c], c, 1, wa[1], wa_sc[:, 1, :], False, False)
+            for z in range(PASSES):
+                tokens_pass(p_bank[c], c, z, wa[z][:], wa_plane[:, z, :], z == 0, False)
 
-        def gains(c0, c1):
-            for c in (c0, c1):
-                nc.scalar.activation(out=pos[c][:], in_=d_ps[c][:], func=ACT.Relu)
-            for c in (c0, c1):
-                nc.scalar.activation(out=root[c][:], in_=pos[c][:], func=ACT.Abs_reciprocal_sqrt, bias=1.0)
-            for c in (c0, c1):
-                nc.scalar.activation(out=gain[c][:], in_=root[c][:], func=ACT.Square)
+        def second_product(c):
+            for z in range(PASSES):
+                moving = xq_codes[c][z][:].bitcast(FP8X4)
+                mx_pass(p_bank[c], wq[z][:], wq_plane[:, z, :], FP4X4, moving, xq_plane[c][z][:], False, z == PASSES - 1)
 
-        def quotient(c, r):
-            cols = slice(CH * r, CH * (r + 1))
-            nc.vector.tensor_tensor(out=quot[c][:, cols], in0=p_ps[c][:, cols], in1=gain[c][:, cols], op=ALU.mult)
+        def positive_part(c):
+            nc.scalar.activation(out=positive[c][:], in_=d_bank[c][:], func=ACT.Relu)
 
-        def add_share(c, r):
-            cols = slice(CH * r, CH * (r + 1))
-            nc.vector.scalar_tensor_tensor(
-                out=y[c][:, r, :], in0=d_ps[c][:, cols], scalar=share[:, r : r + 1], in1=quot[c][:, cols],
-                op0=ALU.mult, op1=ALU.add,
-            )
+        def inverse_root(c):
+            nc.scalar.activation(out=root[c][:], in_=positive[c][:], func=ACT.Abs_reciprocal_sqrt, bias=1.0)
 
-        def quotients(c):
-            nc.vector.tensor_tensor(out=quot[c][:], in0=p_ps[c][:], in1=gain[c][:], op=ALU.mult)
+        def square(c):
+            nc.scalar.activation(out=gain[c][:], in_=root[c][:], func=ACT.Square)
 
-        def finish_by_rows(c):
-            for step in range(PACK + 2):
-                if step < PACK:
-                    quotient(c, step)
-                if step >= 2:
-                    add_share(c, step - 2)
-            store_y(c)
+        def prepare(c):
+            for z in range(PASSES):
+                if z > 0 or c < FIRST_LATE_CHUNK:
+                    round_rows(nc.vector.tensor_copy, xq_bf[c][z], xq_raw[c][z])
+            for z in range(PASSES):
+                quantize(xq_codes[c][z][:], xq_plane[c][z][:], xq_bf[c][z][:])
+            second_product(c)
+            if c + 2 < CHUNKS:
+                first_product(c + 2)
 
         def finish(c):
-            for r in range(PACK):
-                add_share(c, r)
-            store_y(c)
-
-        def store_y(c):
-            nc.sync.dma_start(
-                out=out_0.rearrange("(p r) t -> p r t", r=PACK)[:, :, CH * c : CH * (c + 1)], in_=y[c][:]
-            )
-
-        def quantize_xq(i):
-            quantize(xq_c[i][:], xq_sc[i][:], xq_bf[i][:])
-
-        def round_xq(engine, i):
-            interleave(engine, xq_bf[i][:], xq_raw[i][:])
-
-        def round_y(engine, c):
-            if engine == "gpsimd":
-                nc.gpsimd.tensor_scalar(
-                    out=y_bf[c][:].rearrange("p (t r) -> p t r", r=PACK), in0=y[c][:].rearrange("p r t -> p t r"),
-                    scalar1=1.0, scalar2=-0.0, op0=ALU.mult, op1=ALU.add,
-                )
-            else:
-                interleave(engine, y_bf[c][:], y[c][:])
+            for step in range(PACK + 2):
+                if step < PACK:
+                    cols = span(step, CH)
+                    nc.vector.tensor_tensor(
+                        out=quotient[c][:, cols], in0=p_bank[c][:, cols], in1=gain[c][:, cols], op=ALU.mult
+                    )
+                if step >= 2:
+                    r = step - 2
+                    nc.vector.scalar_tensor_tensor(
+                        out=y[c][:, r, :],
+                        in0=d_bank[c][:, span(r, CH)],
+                        scalar=share[:, r : r + 1],
+                        in1=quotient[c][:, span(r, CH)],
+                        op0=ALU.mult,
+                        op1=ALU.add,
+                    )
+            rows = out_0.rearrange("(p r) t -> p r t", r=PACK)
+            nc.sync.dma_start(out=rows[:, :, span(c, CH)], in_=y[c][:])
 
         def quantize_y(c):
-            quantize(y_c[:, CH * c : CH * (c + 1)], y_sc[:, CH * c : CH * (c + 1)], y_bf[c][:])
+            quantize(y_codes[:, span(c, CH)], y_plane[:, span(c, CH)], y_bf[c][:])
 
-        def store_words(queue, t0, t1):
+        def store_codes(queue, half):
             words = out_1[0].rearrange("p c r -> p (c r)").bitcast(I32)
-            queue.dma_start(out=words[:, t0:t1], in_=y_c[:, t0:t1].bitcast(I32))
+            queue.dma_start(out=words[:, span(half, T // 2)], in_=y_codes[:, span(half, T // 2)].bitcast(I32))
 
         ctx.enter_context(tc.manual_schedule())
 
-        nc.gpsimd.memset(wq_sc_raw[:].bitcast(I32), 0)
-        load_scales(nc.gpsimd, wq_sc_raw, wq_scales, (0,))
-        load_scales(nc.gpsimd, wq_sc_raw, wq_scales, (1,))
-        load_scales(nc.gpsimd, wq_sc_raw, wq_scales, (2,))
-        load_scales(nc.gpsimd, wq_sc_raw, wq_scales, (3,))
-        nc.gpsimd.dma_start(out=share[:], in_=sh.rearrange("(p r) o -> p (r o)", r=PACK))
-        nc.vector.memset(xt_sc[:].bitcast(I32), 0)
-        nc.vector.memset(warm_in[:], 1.0)
-        nc.scalar.activation(out=warm_out[:], in_=warm_in[:], func=ACT.Abs_reciprocal_sqrt)
-        nc.vector.memset(wa_sc_raw[:].bitcast(I32), 0)
-        load_wd(0)
-        load_scales(nc.sync, xt_sc, xt_scales, (0,))
-        load_scales(nc.sync, xt_sc, xt_scales, (1,))
-        load_scales(nc.sync, xt_sc, xt_scales, (2,))
-        load_scales(nc.sync, xt_sc, xt_scales, (3,))
-        load_wd(1)
-        nc.sync.dma_start(out=xt[:].bitcast(I32), in_=xt_words.rearrange("z p b -> p z b").bitcast(I32))
-        nc.sync.dma_start(out=wa_raw[:], in_=wa_words.rearrange("z p n t -> p z (n t)").bitcast(I32))
-        load_scales(nc.sync, wa_sc_raw, wa_scales, (0,))
-        load_scales(nc.sync, wa_sc_raw, wa_scales, (1,))
-        load_scales(nc.sync, wa_sc_raw, wa_scales, (2,))
-        load_scales(nc.sync, wa_sc_raw, wa_scales, (3,))
+        nc.vector.memset(xt_plane[:].bitcast(I32), 0)
+        nc.vector.memset(table_in[:], 1.0)
+        nc.scalar.activation(out=table_out[:], in_=table_in[:], func=ACT.Abs_reciprocal_sqrt)
+        nc.vector.memset(wq_plane_raw[:].bitcast(I32), 0)
+        nc.vector.memset(wa_plane_raw[:].bitcast(I32), 0)
+
         nc.sync.dma_start(out=wq_raw[:].bitcast(I32), in_=wq_words.rearrange("z p b -> p z b").bitcast(I32))
-        load_xq(0)
-        load_xq(1)
-        load_xq(2)
-        load_xq(3)
-        load_xq(4)
-        load_xq(5)
-        load_xq(6)
-        load_xq(7)
-        round_wd("vector", 0, 0, 92)
-        round_wd("scalar", 0, 92, wd_pieces[0][2] // PACK)
-        quantize(wd_c[0][:], wd_sc[0][:], wd_bf[0][:])
-        by_tokens(d_ps[0], 0, 0, wd_c[0], wd_sc[0], True, False)
-        by_tokens(d_ps[1], 1, 0, wd_c[0], wd_sc[0], True, False)
-        round_wd("vector", 1, 0, 92)
-        round_wd("scalar", 1, 92, wd_pieces[1][2] // PACK)
+        load_rows(wd_raw[0], wd, 0, slice(0, N))
+        load_scales(xt_plane, xt_scales)
+        load_rows(wd_raw[1], wd, 1, slice(0, N))
+        nc.sync.dma_start(out=xt[:].bitcast(I32), in_=xt_words.rearrange("z p b -> p z b").bitcast(I32))
+        load_scales(wq_plane_raw, wq_scales)
+        nc.sync.dma_start(out=wa_raw[:], in_=wa_words.rearrange("z p n j -> p z (n j)").bitcast(I32))
+        load_scales(wa_plane_raw, wa_scales)
+        nc.sync.dma_start(out=share[:], in_=sh.rearrange("(p r) o -> p (r o)", r=PACK))
+        for c in range(CHUNKS):
+            for z in range(PASSES):
+                load_rows(xq_raw[c][z], xq, z, span(c, CH))
+
+        for z in range(PASSES):
+            deal_wq(z)
+
+        early, late = range(FIRST_LATE_CHUNK), range(FIRST_LATE_CHUNK, CHUNKS)
+        round_wd(0)
+        quantize(wd_codes[0][:], wd_plane[0][:], wd_bf[0][:])
+        round_wd(1)
         for r in range(PACK):
-            quantize(wd_c[1][:, P * r : P * (r + 1)], wd_sc[1][:, P * r : P * (r + 1)], wd_bf[1][:, 512 * r : 512 * (r + 1)])
-        by_tokens(d_ps[0], 0, 1, wd_c[1], wd_sc[1], False, True)
-        by_tokens(d_ps[1], 1, 1, wd_c[1], wd_sc[1], False, True)
-        by_tokens(d_ps[2], 2, 0, wd_c[0], wd_sc[0], True, False)
-        by_tokens(d_ps[2], 2, 1, wd_c[1], wd_sc[1], False, True)
-        by_tokens(d_ps[3], 3, 0, wd_c[0], wd_sc[0], True, False)
-        by_tokens(d_ps[3], 3, 1, wd_c[1], wd_sc[1], False, True)
-        nc.scalar.activation(out=pos[0][:], in_=d_ps[0][:], func=ACT.Relu)
-        nc.scalar.activation(out=pos[1][:], in_=d_ps[1][:], func=ACT.Relu)
-        nc.scalar.activation(out=root[0][:], in_=pos[0][:], func=ACT.Abs_reciprocal_sqrt, bias=1.0)
-        nc.scalar.activation(out=root[1][:], in_=pos[1][:], func=ACT.Abs_reciprocal_sqrt, bias=1.0)
-        nc.scalar.activation(out=gain[0][:], in_=root[0][:], func=ACT.Square)
-        nc.scalar.activation(out=gain[1][:], in_=root[1][:], func=ACT.Square)
-        deal_scales(wq_sc, wq_sc_raw)
-        deal_wa(0)
-        deal_wa(1)
-        deal_scales(wa_sc, wa_sc_raw)
-        by_tokens(p_ps[0], 0, 0, wa[0], wa_sc[:, 0, :], True, False)
-        by_tokens(p_ps[0], 0, 1, wa[1], wa_sc[:, 1, :], False, False)
-        by_tokens(p_ps[1], 1, 0, wa[0], wa_sc[:, 0, :], True, False)
-        by_tokens(p_ps[1], 1, 1, wa[1], wa_sc[:, 1, :], False, False)
-        deal_wq(0)
-        deal_wq(1)
-        round_xq("vector", 0)
-        quantize_xq(0)
-        by_second_input(0, 0, False, False)
-        round_xq("vector", 1)
-        quantize_xq(1)
-        by_second_input(0, 1, False, True)
-        by_tokens(p_ps[2], 2, 0, wa[0], wa_sc[:, 0, :], True, False)
-        by_tokens(p_ps[2], 2, 1, wa[1], wa_sc[:, 1, :], False, False)
-        round_xq("vector", 2)
-        nc.scalar.activation(out=pos[2][:], in_=d_ps[2][:], func=ACT.Relu)
-        nc.scalar.activation(out=pos[3][:], in_=d_ps[3][:], func=ACT.Relu)
-        nc.scalar.activation(out=root[2][:], in_=pos[2][:], func=ACT.Abs_reciprocal_sqrt, bias=1.0)
-        round_xq("vector", 3)
-        quantize_xq(2)
-        by_second_input(1, 0, False, False)
-        quotients(0)
-        quantize_xq(3)
-        by_second_input(1, 1, False, True)
-        by_tokens(p_ps[3], 3, 0, wa[0], wa_sc[:, 0, :], True, False)
-        by_tokens(p_ps[3], 3, 1, wa[1], wa_sc[:, 1, :], False, False)
-        round_xq("scalar", 4)
-        finish(0)
-        round_xq("vector", 5)
-        quantize_xq(4)
-        by_second_input(2, 0, False, False)
-        nc.scalar.activation(out=gain[2][:], in_=root[2][:], func=ACT.Square)
-        nc.scalar.activation(out=root[3][:], in_=pos[3][:], func=ACT.Abs_reciprocal_sqrt, bias=1.0)
-        quotients(1)
-        quantize_xq(5)
-        by_second_input(2, 1, False, True)
-        round_xq("scalar", 6)
-        finish(1)
-        round_xq("vector", 7)
-        quantize_xq(6)
-        by_second_input(3, 0, False, False)
-        nc.scalar.activation(out=gain[3][:], in_=root[3][:], func=ACT.Square)
-        round_y("scalar", 0)
-        round_y("scalar", 1)
-        quotients(2)
-        quantize_xq(7)
-        by_second_input(3, 1, False, True)
+            quantize(wd_codes[1][:, span(r, P)], wd_plane[1][:, span(r, P)], wd_bf[1][:, span(r, PACK * P)])
+        for chunks in (early, late):
+            for z in range(PASSES):
+                drive_passes(chunks, z)
+
+        for stage in (positive_part, inverse_root, square):
+            for c in early:
+                stage(c)
+        for c in late:
+            positive_part(c)
+        for c in late:
+            inverse_root(c)
+            round_rows(nc.scalar.copy, xq_bf[c][0], xq_raw[c][0])
+            square(c)
+
+        deal_plane(wq_plane, wq_plane_raw)
+        for z in range(PASSES):
+            deal_wa(z)
+        deal_plane(wa_plane, wa_plane_raw)
+        first_product(0)
+        first_product(1)
+
+        last = CHUNKS - 1
+        prepare(0)
+        for c in range(last):
+            prepare(c + 1)
+            finish(c)
+            round_rows(nc.scalar.copy, y_bf[c], y[c])
+
         quantize_y(0)
-        finish(2)
-        round_y("scalar", 2)
         quantize_y(1)
-        store_words(nc.sync, 0 * CH, 2 * CH)
-        finish_by_rows(3)
-        quantize_y(2)
-        store_words(nc.sync, 2 * CH, 3 * CH)
-        round_y("vector", 3)
-        quantize_y(3)
-        store_words(nc.scalar, 3 * CH, 4 * CH)
-        for q in range(4):
+        store_codes(nc.sync, 0)
+        finish(last)
+        quantize_y(last - 1)
+        round_rows(nc.vector.tensor_copy, y_bf[last], y[last])
+        quantize_y(last)
+        store_codes(nc.scalar, 1)
+        for q in range(QUADRANTS):
             queue = nc.sync if q % 2 == 0 else nc.scalar
-            queue.dma_start(
-                out=out_2[0, 4 * q : 4 * q + 4, :].bitcast(I32), in_=y_sc[32 * q : 32 * q + 4, :].bitcast(I32)
-            )
+            queue.dma_start(out=out_2[0, span(q, 4), :].bitcast(I32), in_=y_plane[32 * q : 32 * q + 4, :].bitcast(I32))

@@ -25,6 +25,8 @@ CHUNKS = T // CH
 LINE = 16
 WD_ON_VECTOR = 92
 FIRST_LATE_CHUNK = 2
+SUM_LAG = 2
+STEPS = PACK + SUM_LAG
 
 
 def tile_mix_sum_divided_by_drive_pl_kernel(
@@ -55,8 +57,8 @@ def tile_mix_sum_divided_by_drive_pl_kernel(
         wq_plane = tile("wq_plane", [P, PASSES, N], U8)
         wa_plane = tile("wa_plane", [P, PASSES, N], U8)
         share = tile("share", [P, PACK], F32)
-        table_in = tile("table_in", [P, 1], F32)
-        table_out = tile("table_out", [P, 1], F32)
+        one_in = tile("one_in", [P, 1], F32)
+        one = tile("one", [P, 1], F32)
 
         wd_raw = by_pass("wd_raw", [P, PACK, N], F32)
         wd_bf = by_pass("wd_bf", [P, PACK * N], BF16)
@@ -160,30 +162,31 @@ def tile_mix_sum_divided_by_drive_pl_kernel(
             nc.scalar.activation(out=positive[c][:], in_=d_bank[c][:], func=ACT.Relu)
 
         def inverse_root(c):
-            nc.scalar.activation(out=root[c][:], in_=positive[c][:], func=ACT.Abs_reciprocal_sqrt, bias=1.0)
+            nc.scalar.activation(out=root[c][:], in_=positive[c][:], func=ACT.Abs_reciprocal_sqrt, bias=one[:])
 
         def square(c):
             nc.scalar.activation(out=gain[c][:], in_=root[c][:], func=ACT.Square)
 
-        def prepare(c):
-            for z in range(PASSES):
-                if z > 0 or c < FIRST_LATE_CHUNK:
-                    round_rows(nc.vector.tensor_copy, xq_bf[c][z], xq_raw[c][z])
-            for z in range(PASSES):
-                quantize(xq_codes[c][z][:], xq_plane[c][z][:], xq_bf[c][z][:])
+        def round_xq(copy, c, z):
+            round_rows(copy, xq_bf[c][z], xq_raw[c][z])
+
+        def quantize_xq(c, z):
+            quantize(xq_codes[c][z][:], xq_plane[c][z][:], xq_bf[c][z][:])
+
+        def close_p(c):
             second_product(c)
             if c + 2 < CHUNKS:
                 first_product(c + 2)
 
-        def finish(c):
-            for step in range(PACK + 2):
+        def finish(c, steps):
+            for step in steps:
                 if step < PACK:
                     cols = span(step, CH)
                     nc.vector.tensor_tensor(
                         out=quotient[c][:, cols], in0=p_bank[c][:, cols], in1=gain[c][:, cols], op=ALU.mult
                     )
-                if step >= 2:
-                    r = step - 2
+                if step >= SUM_LAG:
+                    r = step - SUM_LAG
                     nc.vector.scalar_tensor_tensor(
                         out=y[c][:, r, :],
                         in0=d_bank[c][:, span(r, CH)],
@@ -192,6 +195,8 @@ def tile_mix_sum_divided_by_drive_pl_kernel(
                         op0=ALU.mult,
                         op1=ALU.add,
                     )
+
+        def store_y(c):
             rows = out_0.rearrange("(p r) t -> p r t", r=PACK)
             nc.sync.dma_start(out=rows[:, :, span(c, CH)], in_=y[c][:])
 
@@ -205,26 +210,29 @@ def tile_mix_sum_divided_by_drive_pl_kernel(
         ctx.enter_context(tc.manual_schedule())
 
         nc.vector.memset(xt_plane[:].bitcast(I32), 0)
-        nc.vector.memset(table_in[:], 1.0)
-        nc.scalar.activation(out=table_out[:], in_=table_in[:], func=ACT.Abs_reciprocal_sqrt)
-        nc.vector.memset(wq_plane_raw[:].bitcast(I32), 0)
+        nc.vector.memset(one_in[:], 1.0)
+        nc.scalar.activation(out=one[:], in_=one_in[:], func=ACT.Abs_reciprocal_sqrt)
         nc.vector.memset(wa_plane_raw[:].bitcast(I32), 0)
+        nc.vector.memset(wq_plane_raw[:].bitcast(I32), 0)
 
-        nc.sync.dma_start(out=wq_raw[:].bitcast(I32), in_=wq_words.rearrange("z p b -> p z b").bitcast(I32))
+        def load_xq(c, z):
+            load_rows(xq_raw[c][z], xq, z, span(c, CH))
+
         load_rows(wd_raw[0], wd, 0, slice(0, N))
         load_scales(xt_plane, xt_scales)
         load_rows(wd_raw[1], wd, 1, slice(0, N))
         nc.sync.dma_start(out=xt[:].bitcast(I32), in_=xt_words.rearrange("z p b -> p z b").bitcast(I32))
-        load_scales(wq_plane_raw, wq_scales)
         nc.sync.dma_start(out=wa_raw[:], in_=wa_words.rearrange("z p n j -> p z (n j)").bitcast(I32))
         load_scales(wa_plane_raw, wa_scales)
-        nc.sync.dma_start(out=share[:], in_=sh.rearrange("(p r) o -> p (r o)", r=PACK))
-        for c in range(CHUNKS):
+        nc.sync.dma_start(out=wq_raw[:].bitcast(I32), in_=wq_words.rearrange("z p b -> p z b").bitcast(I32))
+        load_xq(0, 0)
+        load_scales(wq_plane_raw, wq_scales)
+        load_xq(0, 1)
+        for c in range(1, CHUNKS):
             for z in range(PASSES):
-                load_rows(xq_raw[c][z], xq, z, span(c, CH))
-
-        for z in range(PASSES):
-            deal_wq(z)
+                load_xq(c, z)
+            if c == 1:
+                nc.sync.dma_start(out=share[:], in_=sh.rearrange("(p r) o -> p (r o)", r=PACK))
 
         early, late = range(FIRST_LATE_CHUNK), range(FIRST_LATE_CHUNK, CHUNKS)
         round_wd(0)
@@ -243,29 +251,43 @@ def tile_mix_sum_divided_by_drive_pl_kernel(
             positive_part(c)
         for c in late:
             inverse_root(c)
-            round_rows(nc.scalar.copy, xq_bf[c][0], xq_raw[c][0])
+            round_xq(nc.scalar.copy, c, 0)
             square(c)
 
-        deal_plane(wq_plane, wq_plane_raw)
         for z in range(PASSES):
             deal_wa(z)
         deal_plane(wa_plane, wa_plane_raw)
         first_product(0)
         first_product(1)
+        for z in range(PASSES):
+            deal_wq(z)
+        round_xq(nc.vector.tensor_copy, 0, 0)
+        deal_plane(wq_plane, wq_plane_raw)
+        round_xq(nc.vector.tensor_copy, 0, 1)
+        for z in range(PASSES):
+            quantize_xq(0, z)
+        close_p(0)
 
         last = CHUNKS - 1
-        prepare(0)
         for c in range(last):
-            prepare(c + 1)
-            finish(c)
+            if c + 1 in early:
+                round_xq(nc.vector.tensor_copy, c + 1, 0)
+            round_xq(nc.vector.tensor_copy, c + 1, 1)
+            quantize_xq(c + 1, 0)
+            finish(c, range(1))
+            quantize_xq(c + 1, 1)
+            close_p(c + 1)
+            finish(c, range(1, STEPS))
+            store_y(c)
             round_rows(nc.scalar.copy, y_bf[c], y[c])
+        finish(last, range(STEPS))
+        store_y(last)
 
         quantize_y(0)
         quantize_y(1)
         store_codes(nc.sync, 0)
-        finish(last)
-        quantize_y(last - 1)
         round_rows(nc.vector.tensor_copy, y_bf[last], y[last])
+        quantize_y(2)
         quantize_y(last)
         store_codes(nc.scalar, 1)
         for q in range(QUADRANTS):

from contextlib import ExitStack

import concourse.mybir as mybir

K, T, N = 1024, 512, 512
FLOPS = 3 * 2 * K * N * T

F32 = mybir.dt.float32
BF16 = mybir.dt.bfloat16
I32 = mybir.dt.int32
U32 = mybir.dt.uint32
U8 = mybir.dt.uint8
FP8X4 = mybir.dt.float8_e4m3fn_x4
FP4X4 = mybir.dt.float4_e2m1fn_x4
ALU = mybir.AluOpType
ACT = mybir.ActivationFunctionType

P = 128
PACK = 4
K_PASS = P * PACK
PASSES = K // K_PASS
QUADRANTS = 4
CH = 128
CHUNKS = T // CH
LINE = 16
WD_ON_VECTOR = 92
FIRST_LATE_CHUNK = 2
SUM_LAG = 2
STEPS = PACK + SUM_LAG


def tile_mix_sum_divided_by_drive_pl_kernel(
    tc, xt_words, xt_scales, wa_words, wa_scales, xq, wq_words, wq_scales, wd, sh, out_0, out_1, out_2
):
    nc = tc.nc
    with ExitStack() as ctx:
        sbuf = ctx.enter_context(tc.tile_pool(name="sbuf", bufs=1))
        psum = ctx.enter_context(tc.psum_pool(name="psum", bufs=1))

        def tile(name, shape, dtype):
            return sbuf.tile(shape, dtype, name=name, align_bytes=64)

        def by_pass(name, shape, dtype):
            return [tile("%s%d" % (name, z), shape, dtype) for z in range(PASSES)]

        def by_chunk(name, shape, dtype):
            return [tile("%s%d" % (name, c), shape, dtype) for c in range(CHUNKS)]

        xt = tile("xt", [P, PASSES, 2 * T], U8)
        xt_plane = tile("xt_plane", [P, PASSES, T], U8)
        wq_raw = tile("wq_raw", [P, PASSES, 2 * N], U8)
        wq_plane_raw = tile("wq_plane_raw", [P, PASSES, N], U8)
        wa_raw = tile("wa_raw", [P, PASSES, N], I32)
        wa_plane_raw = tile("wa_plane_raw", [P, PASSES, N], U8)
        wq = by_pass("wq", [P, 2 * N], U8)
        wa = by_pass("wa", [P, N], U32)
        wq_plane = tile("wq_plane", [P, PASSES, N], U8)
        wa_plane = tile("wa_plane", [P, PASSES, N], U8)
        share = tile("share", [P, PACK], F32)
        one_in = tile("one_in", [P, 1], F32)
        one = tile("one", [P, 1], F32)

        wd_raw = by_pass("wd_raw", [P, PACK, N], F32)
        wd_bf = by_pass("wd_bf", [P, PACK * N], BF16)
        wd_codes = by_pass("wd_codes", [P, N], U32)
        wd_plane = by_pass("wd_plane", [P, N], U8)
        xq_raw = [by_pass("xq_raw%d_" % c, [P, PACK, CH], F32) for c in range(CHUNKS)]
        xq_bf = [by_pass("xq_bf%d_" % c, [P, PACK * CH], BF16) for c in range(CHUNKS)]
        xq_codes = [by_pass("xq_codes%d_" % c, [P, CH], U32) for c in range(CHUNKS)]
        xq_plane = [by_pass("xq_plane%d_" % c, [P, CH], U8) for c in range(CHUNKS)]

        positive = by_chunk("positive", [P, PACK * CH], F32)
        root = by_chunk("root", [P, PACK * CH], F32)
        gain = by_chunk("gain", [P, PACK * CH], F32)
        quotient = by_chunk("quotient", [P, PACK * CH], F32)
        y = by_chunk("y", [P, PACK, CH], F32)
        y_bf = by_chunk("y_bf", [P, PACK * CH], BF16)
        y_codes = tile("y_codes", [P, T], U32)
        y_plane = tile("y_plane", [P, T], U8)

        d_bank = [psum.tile([P, PACK * CH], F32, name="d_bank%d" % c) for c in range(CHUNKS)]
        p_bank = [psum.tile([P, PACK * CH], F32, name="p_bank%d" % c) for c in range(CHUNKS)]

        def span(i, width):
            return slice(width * i, width * (i + 1))

        def load_scales(plane, scales):
            for q in range(QUADRANTS):
                nc.sync.dma_start(
                    out=plane[32 * q : 32 * q + 4, :, :].bitcast(I32),
                    in_=scales[:, span(q, 4), :].rearrange("z r c -> r z c").bitcast(I32),
                )

        def load_rows(raw, matrix, z, cols):
            rows = matrix[span(z, K_PASS), :].rearrange("(p j) c -> p j c", j=PACK)
            nc.sync.dma_start(out=raw[:], in_=rows[:, :, cols])

        def deal_plane(plane, raw):
            nc.vector.tensor_copy(
                out=plane[:].rearrange("p z (r a b) -> p z a r b", r=PACK, b=LINE),
                in_=raw[:].rearrange("p z (a b r) -> p z a r b", r=PACK, b=LINE),
            )

        def deal_wq(z):
            nc.vector.tensor_copy(
                out=wq[z][:].rearrange("p (r a b e) -> p a r b e", r=PACK, b=LINE // 2, e=2),
                in_=wq_raw[:, z, :].rearrange("p (a b r e) -> p a r b e", r=PACK, b=LINE // 2, e=2),
            )

        def deal_wa(z):
            nc.vector.tensor_copy(
                out=wa[z][:].bitcast(I32).rearrange("p (r a b) -> p a r b", r=PACK, b=LINE // 4),
                in_=wa_raw[:, z, :].rearrange("p (a b r) -> p a r b", r=PACK, b=LINE // 4),
            )

        def round_wd(z):
            src = wd_raw[z][:].rearrange("p j (m r) -> p m j r", r=PACK)
            dst = wd_bf[z][:].rearrange("p (r m j) -> p m j r", r=PACK, j=PACK)
            nc.vector.tensor_copy(out=dst[:, :WD_ON_VECTOR], in_=src[:, :WD_ON_VECTOR])
            nc.scalar.copy(out=dst[:, WD_ON_VECTOR:], in_=src[:, WD_ON_VECTOR:])

        def round_rows(copy, dst, src):
            copy(
                out=dst[:].rearrange("p (g i j) -> p g j i", i=4, j=PACK),
                in_=src[:].rearrange("p j (g i) -> p g j i", i=4),
            )

        def quantize(codes, plane, values):
            nc.vector.quantize_mx(out=codes.bitcast(FP8X4), scales=plane, in_=values)

        def mx_pass(bank, weights, weights_plane, weights_dtype, moving, moving_plane, start, stop):
            width = weights.shape[1] // PACK
            for r in range(PACK):
                nc.tensor.matmul_mx(
                    out=bank[:, span(r, CH)],
                    lhsT=weights[:, span(r, width)].bitcast(weights_dtype),
                    lhsT_scale=weights_plane[:, span(r, P)],
                    rhs=moving,
                    rhs_scale=moving_plane,
                    start=(start and r == 0),
                    stop=(stop and r == PACK - 1),
                )

        def tokens_pass(bank, c, z, weights, weights_plane, start, stop):
            moving = xt[:, z, span(c, 2 * CH)].bitcast(FP4X4)
            mx_pass(bank, weights, weights_plane, FP8X4, moving, xt_plane[:, z, span(c, CH)], start, stop)

        def drive_passes(chunks, z):
            for c in chunks:
                tokens_pass(d_bank[c], c, z, wd_codes[z][:], wd_plane[z][:], z == 0, z == PASSES - 1)

        def first_product(c):
            for z in range(PASSES):
                tokens_pass(p_bank[c], c, z, wa[z][:], wa_plane[:, z, :], z == 0, False)

        def second_product(c):
            for z in range(PASSES):
                moving = xq_codes[c][z][:].bitcast(FP8X4)
                mx_pass(p_bank[c], wq[z][:], wq_plane[:, z, :], FP4X4, moving, xq_plane[c][z][:], False, z == PASSES - 1)

        def positive_part(c):
            nc.scalar.activation(out=positive[c][:], in_=d_bank[c][:], func=ACT.Relu)

        def inverse_root(c):
            nc.scalar.activation(out=root[c][:], in_=positive[c][:], func=ACT.Abs_reciprocal_sqrt, bias=one[:])

        def square(c):
            nc.scalar.activation(out=gain[c][:], in_=root[c][:], func=ACT.Square)

        def round_xq(copy, c, z):
            round_rows(copy, xq_bf[c][z], xq_raw[c][z])

        def quantize_xq(c, z):
            quantize(xq_codes[c][z][:], xq_plane[c][z][:], xq_bf[c][z][:])

        def close_p(c):
            second_product(c)
            if c + 2 < CHUNKS:
                first_product(c + 2)

        def finish(c, steps):
            for step in steps:
                if step < PACK:
                    cols = span(step, CH)
                    nc.vector.tensor_tensor(
                        out=quotient[c][:, cols], in0=p_bank[c][:, cols], in1=gain[c][:, cols], op=ALU.mult
                    )
                if step >= SUM_LAG:
                    r = step - SUM_LAG
                    nc.vector.scalar_tensor_tensor(
                        out=y[c][:, r, :],
                        in0=d_bank[c][:, span(r, CH)],
                        scalar=share[:, r : r + 1],
                        in1=quotient[c][:, span(r, CH)],
                        op0=ALU.mult,
                        op1=ALU.add,
                    )

        def store_y(c):
            rows = out_0.rearrange("(p r) t -> p r t", r=PACK)
            nc.sync.dma_start(out=rows[:, :, span(c, CH)], in_=y[c][:])

        def quantize_y(c):
            quantize(y_codes[:, span(c, CH)], y_plane[:, span(c, CH)], y_bf[c][:])

        def store_codes(queue, half):
            words = out_1[0].rearrange("p c r -> p (c r)").bitcast(I32)
            queue.dma_start(out=words[:, span(half, T // 2)], in_=y_codes[:, span(half, T // 2)].bitcast(I32))

        ctx.enter_context(tc.manual_schedule())

        nc.vector.memset(xt_plane[:].bitcast(I32), 0)
        nc.vector.memset(one_in[:], 1.0)
        nc.scalar.activation(out=one[:], in_=one_in[:], func=ACT.Abs_reciprocal_sqrt)
        nc.vector.memset(wa_plane_raw[:].bitcast(I32), 0)
        nc.vector.memset(wq_plane_raw[:].bitcast(I32), 0)

        def load_xq(c, z):
            load_rows(xq_raw[c][z], xq, z, span(c, CH))

        load_rows(wd_raw[0], wd, 0, slice(0, N))
        load_scales(xt_plane, xt_scales)
        load_rows(wd_raw[1], wd, 1, slice(0, N))
        nc.sync.dma_start(out=xt[:].bitcast(I32), in_=xt_words.rearrange("z p b -> p z b").bitcast(I32))
        nc.sync.dma_start(out=wa_raw[:], in_=wa_words.rearrange("z p n j -> p z (n j)").bitcast(I32))
        load_scales(wa_plane_raw, wa_scales)
        nc.sync.dma_start(out=wq_raw[:].bitcast(I32), in_=wq_words.rearrange("z p b -> p z b").bitcast(I32))
        load_xq(0, 0)
        load_scales(wq_plane_raw, wq_scales)
        load_xq(0, 1)
        for c in range(1, CHUNKS):
            for z in range(PASSES):
                load_xq(c, z)
            if c == 1:
                nc.sync.dma_start(out=share[:], in_=sh.rearrange("(p r) o -> p (r o)", r=PACK))

        early, late = range(FIRST_LATE_CHUNK), range(FIRST_LATE_CHUNK, CHUNKS)
        round_wd(0)
        quantize(wd_codes[0][:], wd_plane[0][:], wd_bf[0][:])
        round_wd(1)
        for r in range(PACK):
            quantize(wd_codes[1][:, span(r, P)], wd_plane[1][:, span(r, P)], wd_bf[1][:, span(r, PACK * P)])
        for chunks in (early, late):
            for z in range(PASSES):
                drive_passes(chunks, z)

        for stage in (positive_part, inverse_root, square):
            for c in early:
                stage(c)
        for c in late:
            positive_part(c)
        for c in late:
            inverse_root(c)
            round_xq(nc.scalar.copy, c, 0)
            square(c)

        for z in range(PASSES):
            deal_wa(z)
        deal_plane(wa_plane, wa_plane_raw)
        first_product(0)
        first_product(1)
        for z in range(PASSES):
            deal_wq(z)
        round_xq(nc.vector.tensor_copy, 0, 0)
        deal_plane(wq_plane, wq_plane_raw)
        round_xq(nc.vector.tensor_copy, 0, 1)
        for z in range(PASSES):
            quantize_xq(0, z)
        close_p(0)

        last = CHUNKS - 1
        for c in range(last):
            if c + 1 in early:
                round_xq(nc.vector.tensor_copy, c + 1, 0)
            round_xq(nc.vector.tensor_copy, c + 1, 1)
            quantize_xq(c + 1, 0)
            finish(c, range(1))
            quantize_xq(c + 1, 1)
            close_p(c + 1)
            finish(c, range(1, STEPS))
            store_y(c)
            round_rows(nc.scalar.copy, y_bf[c], y[c])
        finish(last, range(STEPS))
        store_y(last)

        quantize_y(0)
        quantize_y(1)
        store_codes(nc.sync, 0)
        round_rows(nc.vector.tensor_copy, y_bf[last], y[last])
        quantize_y(2)
        quantize_y(last)
        store_codes(nc.scalar, 1)
        for q in range(QUADRANTS):
            queue = nc.sync if q % 2 == 0 else nc.scalar
            queue.dma_start(out=out_2[0, span(q, 4), :].bitcast(I32), in_=y_plane[32 * q : 32 * q + 4, :].bitcast(I32))
